import numpy as np, ml_dtypes
CORES = [7,391,135,263,15,399,143,271]
N = 8
T, G, CAP = 4096, 4096, 512
def entries(a): return a.T.reshape(-1)
def pack(v, P): return np.ascontiguousarray(np.asarray(v, np.int32).reshape(-1, P).T)
def lists(rng, how):
    S = rng.integers(0, T, (N, 2 * CAP)); P = np.stack([rng.permutation(G)[:2 * CAP] for r in range(N)])
    if how == "alike": S[:] = rng.integers(0, T, (N, 1))
    if how == "edge":
        S = np.where(rng.random((N, 2 * CAP)) < 0.5, 0, T - 1); S[:, [0, CAP]] = 0; S[:, [1, CAP + 1]] = T - 1
        P[:, 1:-1] = np.stack([1 + rng.permutation(G - 2)[:2 * CAP - 2] for r in range(N)]); P[0::2, 0], P[0::2, -1] = 0, G - 1; P[1::2, 0], P[1::2, -1] = G - 1, 0
    if how == "mixed": P = np.stack([rng.permutation(2 * CAP) for r in range(N)]); P[1::2] += G - 2 * CAP
    if how == "sorted":
        S2, P2 = [-np.sort(-A.reshape(N, 2, CAP), axis=2).reshape(N, 2 * CAP) for A in (S, P)]; S, P = -np.sort(-S, axis=1), -np.sort(-P, axis=1)
        S[1::3], P[1::3] = S[1::3, ::-1].copy(), P[1::3, ::-1].copy(); S[2::3], P[2::3] = S2[2::3], P2[2::3]
    return {"snd": np.stack([pack(s, 16) for s in S]), "plc": np.stack([pack(q, 16) for q in P])}
def setup_inputs(rng):
    return dict({"x": rng.standard_normal((N, 128, T), dtype=np.float32).astype(ml_dtypes.bfloat16), "gh": rng.standard_normal((N, 128, G), dtype=np.float32).astype(ml_dtypes.bfloat16)}, **lists(rng, "uniform"))
def setup_inputs_alike(rng):
    d = setup_inputs(rng); d.update(lists(rng, "alike"))
    for k in ("x", "gh"): d[k] = (d[k].astype(np.float32) * 1048576.0).astype(d[k].dtype)
    return d
def setup_inputs_edge(rng):
    d = setup_inputs(rng); d.update(lists(rng, "edge"))
    for k in ("x", "gh"): d[k] = (d[k].astype(np.float32) * (1 / 1024.0)).astype(d[k].dtype)
    return d
def setup_inputs_mixed(rng):
    d = setup_inputs(rng); d.update(lists(rng, "mixed"))
    return d
def setup_inputs_sorted(rng):
    d = setup_inputs(rng); d.update(lists(rng, "sorted"))
    return d
def setup_inputs_zeros(rng):
    d = setup_inputs(rng); d.update(lists(rng, "zeros"))
    for r in range(N): d["x"][r][:, entries(d["snd"][r])[::2]] = 0
    return d
def check_inputs(x):
    bad = []
    if x["snd"].min() < 0 or x["snd"].max() >= T: bad.append("snd out of range")
    if x["plc"].min() < 0 or x["plc"].max() >= G: bad.append("plc out of range")
    if any(len(np.unique(a)) != a.size for a in x["plc"]): bad.append("a place is named twice")
    return bad
def reference(x, gh, snd, plc):
    y = gh.copy()
    for r in range(N):
        S = entries(snd[r]); lo, hi = (r - 1) % N, (r + 1) % N
        y[lo][:, entries(plc[lo])[CAP:]] = x[r][:, S[:CAP]]
        y[hi][:, entries(plc[hi])[:CAP]] = x[r][:, S[CAP:]]
    return {"y": y}

@@ -1,0 +1,144 @@
+import numpy as np
+from concourse.mybir import dt, AluOpType
+
+PIECES = [256, 256]
+XC, HALF, LP, LW = 4096, 512, 16, 64
+ALL_CORES = 512
+
+SCRATCH = {
+    "xs": ("sbuf", [128, XC], "bfloat16"),
+    "gs": ("sbuf", [128, XC], "bfloat16"),
+    "sdir": ("sbuf", [128, HALF], "bfloat16"),
+    "rdir": ("sbuf", [128, HALF], "bfloat16"),
+    "li": ("sbuf", [128, 2 * LW], "int32"),
+    "lf": ("sbuf", [128, 2 * LW], "float32"),
+    "offs": ("sbuf", [128, 2 * LW], "uint16"),
+    "dif": ("sbuf", [128, 128], "float32"),
+    "rep": ("sbuf", [128, 128], "float32"),
+    "pl": ("psum", [128, 512], "float32"),
+}
+SEMAPHORES = ["lst", "xld", "gld", "dif_s", "rep_s", "lf_s", "pl_s", "off_s", "gdir", "adir", "sct", "sent", "stored"]
+for _k, _w in enumerate(PIECES):
+    SCRATCH["snd%d" % _k] = ("sbuf", [128, _w], "bfloat16")
+    SCRATCH["via%d" % _k] = ("sbuf", [128, _w], "bfloat16")
+    SCRATCH["rcv%d" % _k] = ("sbuf", [128, _w], "bfloat16")
+    SEMAPHORES += ["gat%d" % _k, "via_s%d" % _k, "arr%d" % _k]
+
+_PLAN = {}
+
+
+def nbits(m):
+    return bin(m).count("1")
+
+
+def relay_for(s, d, T, topo):
+    for c in range(ALL_CORES):
+        if topo.host(c) == topo.host(s) or topo.rack(topo.host(c)) != topo.rack(topo.host(s)):
+            continue
+        if T.rank_of(c) is not None or topo.chip(c) != topo.chip(d) or topo.die(c) != topo.die(s):
+            continue
+        if not (topo.may_write(s, c) and topo.may_write(c, d)):
+            continue
+        if any(topo.mates(c, q) and topo.may_write(c, q) for q in range(ALL_CORES)):
+            continue
+        return c
+    raise ValueError("no relay from %d to %d" % (s, d))
+
+
+def plan(T, topo):
+    if not _PLAN:
+        cores = list(T.cores)
+        n = len(cores)
+        _PLAN["relays"], _PLAN["via"], _PLAN["far"] = {}, {}, {}
+        for r, s in enumerate(cores):
+            nb = [cores[(r - 1) % n], cores[(r + 1) % n]]
+            far = [k for k in (0, 1) if not topo.may_write(s, nb[k])]
+            assert len(far) == 1
+            c = relay_for(s, nb[far[0]], T, topo)
+            assert c not in _PLAN["relays"]
+            _PLAN["far"][r] = far[0]
+            _PLAN["via"][s] = c
+            _PLAN["relays"][c] = (s, nb[far[0]])
+    return _PLAN
+
+
+def run_relay(g, core, T, topo, s, d):
+    rid, pid = topo.addr(d, core)
+    m_in, m_out = topo.mask(s, core), topo.mask(core, d)
+    for k in range(len(PIECES)):
+        g.wait_ge(T.sem["via_s%d" % k], nbits(m_in))
+        g.remote_dma(T["rcv%d" % k][:], T["via%d" % k][:], T.sem["arr%d" % k], T.sem.sent, pid, rid, m_out)
+    g.wait_ge(T.sem.sent, nbits(m_out) * len(PIECES))
+
+
+def rank_program(g, core, T, topo):
+    p = plan(T, topo)
+    if core in p["relays"]:
+        s, d = p["relays"][core]
+        return run_relay(g, core, T, topo, s, d)
+    r = T.rank_of(core)
+    if r is None:
+        return
+    cores = list(T.cores)
+    n = len(cores)
+    nb = [cores[(r - 1) % n], cores[(r + 1) % n]]
+    far = p["far"][r]
+    near = 1 - far
+    hc = LW // 2
+    v, S = g.vector, T.sem
+
+    g.sync.dma_start(T.li[0:LP, 0:LW], T.snd[:]).then_inc(S.lst, 16)
+    g.scalar.dma_start(T.li[0:LP, LW:2 * LW], T.plc[:]).then_inc(S.lst, 16)
+    g.sync.dma_start(T.xs[0:64, :], T.x[0:64, :]).then_inc(S.xld, 16)
+    g.scalar.dma_start(T.xs[64:128, :], T.x[64:128, :]).then_inc(S.xld, 16)
+    g.sync.dma_start(T.gs[0:64, :], T.gh[0:64, :]).then_inc(S.gld, 16)
+    g.scalar.dma_start(T.gs[64:128, :], T.gh[64:128, :]).then_inc(S.gld, 16)
+
+    g.iota(T.dif[0:LP, :], [[0, 128 // LP], [1, LP]], 0, -1, allow_small_or_imprecise_dtypes=True).then_inc(S.dif_s, 1)
+    v.wait_ge(S.dif_s, 1)
+    v.tensor_scalar(T.rep[0:LP, :], T.dif[0:LP, :], 0.0, None, AluOpType.is_equal).then_inc(S.rep_s, 1)
+    v.wait_ge(S.lst, 32)
+    v.tensor_copy(T.lf[0:LP, :], T.li[0:LP, :]).then_inc(S.lf_s, 1)
+    g.tensor.wait_ge(S.rep_s, 1)
+    g.tensor.wait_ge(S.lf_s, 1)
+    g.tensor.matmul(T.pl[:, 0:2 * LW], T.rep[0:LP, :], T.lf[0:LP, :], True, True).then_inc(S.pl_s, 1)
+    v.wait_ge(S.pl_s, 1)
+    v.tensor_copy(T.offs[:], T.pl[:, 0:2 * LW]).then_inc(S.off_s, 1)
+
+    v.wait_ge(S.off_s, 1)
+    v.wait_ge(S.xld, 32)
+    o = far * hc
+    for k, w in enumerate(PIECES):
+        v.tensor_copy(T["snd%d" % k][:], T.xs[:, :].indirect(T.offs[:, o:o + w // LP])).then_inc(S["gat%d" % k], 1)
+        o += w // LP
+    v.tensor_copy(T.sdir[:], T.xs[:, :].indirect(T.offs[:, near * hc:(near + 1) * hc])).then_inc(S.gdir, 1)
+
+    via = p["via"][core]
+    rid, pid = topo.addr(via, core)
+    m = topo.mask(core, via)
+    for k in range(len(PIECES)):
+        g.wait_ge(S["gat%d" % k], 1)
+        g.remote_dma(T["via%d" % k][:], T["snd%d" % k][:], S["via_s%d" % k], S.sent, pid, rid, m)
+    rid, pid = topo.addr(nb[near], core)
+    md = topo.mask(core, nb[near])
+    g.wait_ge(S.gdir, 1)
+    g.remote_dma(T.rdir[:], T.sdir[:], S.adir, S.sent, pid, rid, md)
+
+    v.wait_ge(S.gld, 32)
+    v.wait_ge(S.adir, nbits(topo.mask(nb[near], core)))
+    v.tensor_copy(T.gs[:, :].indirect(T.offs[:, LW + near * hc:LW + (near + 1) * hc]), T.rdir[:]).then_inc(S.sct, 1)
+    o = LW + far * hc
+    last = p["via"][nb[far]]
+    for k, w in enumerate(PIECES):
+        v.wait_ge(S["arr%d" % k], nbits(topo.mask(last, core)))
+        v.wait_ge(S.sct, 1 + k)
+        v.tensor_copy(T.gs[:, :].indirect(T.offs[:, o:o + w // LP]), T["rcv%d" % k][:]).then_inc(S.sct, 1)
+        o += w // LP
+
+    done = 1 + len(PIECES)
+    g.sync.wait_ge(S.sct, done)
+    g.sync.dma_start(T.y[0:64, :], T.gs[0:64, :]).then_inc(S.stored, 16)
+    g.scalar.wait_ge(S.sct, done)
+    g.scalar.dma_start(T.y[64:128, :], T.gs[64:128, :]).then_inc(S.stored, 16)
+    g.wait_ge(S.sent, nbits(m) * len(PIECES) + nbits(md))
+    g.wait_ge(S.stored, 32)

@@ -1,28 +1,35 @@
 import numpy as np
-from concourse.mybir import dt, AluOpType
+from concourse.mybir import dt, AluOpType, ActivationFunctionType
 
-PIECES = [256, 256]
+PIECES = [(128, 0), (192, 1), (320, None), (192, 0), (192, None)]
+SCATTERS = [2, 4, 0, 1, 3]
 XC, HALF, LP, LW = 4096, 512, 16, 64
 ALL_CORES = 512
+RELAYS = 2
 
 SCRATCH = {
     "xs": ("sbuf", [128, XC], "bfloat16"),
     "gs": ("sbuf", [128, XC], "bfloat16"),
-    "sdir": ("sbuf", [128, HALF], "bfloat16"),
-    "rdir": ("sbuf", [128, HALF], "bfloat16"),
     "li": ("sbuf", [128, 2 * LW], "int32"),
     "lf": ("sbuf", [128, 2 * LW], "float32"),
     "offs": ("sbuf", [128, 2 * LW], "uint16"),
     "dif": ("sbuf", [128, 128], "float32"),
     "rep": ("sbuf", [128, 128], "float32"),
+    "nz": ("sbuf", [128, 1], "float32"),
     "pl": ("psum", [128, 512], "float32"),
 }
-SEMAPHORES = ["lst", "xld", "gld", "dif_s", "rep_s", "lf_s", "pl_s", "off_s", "gdir", "adir", "sct", "sent", "stored"]
-for _k, _w in enumerate(PIECES):
+SEMAPHORES = ["lst", "xld", "gld", "dif_s", "rep_s", "lf_s", "pl_s", "off_s", "nz_s", "sct", "sent", "stored"]
+START = []
+_at = {True: 0, False: 0}
+for _k, (_w, _r) in enumerate(PIECES):
+    START.append(_at[_r is None])
+    _at[_r is None] += _w
     SCRATCH["snd%d" % _k] = ("sbuf", [128, _w], "bfloat16")
-    SCRATCH["via%d" % _k] = ("sbuf", [128, _w], "bfloat16")
     SCRATCH["rcv%d" % _k] = ("sbuf", [128, _w], "bfloat16")
-    SEMAPHORES += ["gat%d" % _k, "via_s%d" % _k, "arr%d" % _k]
+    SEMAPHORES += ["gat%d" % _k, "arr%d" % _k]
+    if _r is not None:
+        SCRATCH["via%d" % _k] = ("sbuf", [128, _w], "bfloat16")
+        SEMAPHORES.append("via_s%d" % _k)
 
 _PLAN = {}
 
@@ -31,18 +38,22 @@ def nbits(m):
     return bin(m).count("1")
 
 
-def relay_for(s, d, T, topo):
+def relays_for(s, d, T, topo):
+    found = [None, None]
     for c in range(ALL_CORES):
         if topo.host(c) == topo.host(s) or topo.rack(topo.host(c)) != topo.rack(topo.host(s)):
             continue
-        if T.rank_of(c) is not None or topo.chip(c) != topo.chip(d) or topo.die(c) != topo.die(s):
+        if T.rank_of(c) is not None or topo.chip(c) != topo.chip(d):
             continue
         if not (topo.may_write(s, c) and topo.may_write(c, d)):
             continue
         if any(topo.mates(c, q) and topo.may_write(c, q) for q in range(ALL_CORES)):
             continue
-        return c
-    raise ValueError("no relay from %d to %d" % (s, d))
+        i = 0 if topo.die(c) == topo.die(s) else 1
+        if found[i] is None:
+            found[i] = c
+    assert found[0] is not None and found[1] is not None
+    return found
 
 
 def plan(T, topo):
@@ -54,28 +65,32 @@ def plan(T, topo):
             nb = [cores[(r - 1) % n], cores[(r + 1) % n]]
             far = [k for k in (0, 1) if not topo.may_write(s, nb[k])]
             assert len(far) == 1
-            c = relay_for(s, nb[far[0]], T, topo)
-            assert c not in _PLAN["relays"]
+            via = relays_for(s, nb[far[0]], T, topo)
             _PLAN["far"][r] = far[0]
-            _PLAN["via"][s] = c
-            _PLAN["relays"][c] = (s, nb[far[0]])
+            _PLAN["via"][s] = via
+            for i, c in enumerate(via):
+                assert c not in _PLAN["relays"]
+                _PLAN["relays"][c] = (s, nb[far[0]], i)
     return _PLAN
 
 
-def run_relay(g, core, T, topo, s, d):
+def run_relay(g, core, T, topo, s, d, i):
     rid, pid = topo.addr(d, core)
     m_in, m_out = topo.mask(s, core), topo.mask(core, d)
-    for k in range(len(PIECES)):
-        g.wait_ge(T.sem["via_s%d" % k], nbits(m_in))
-        g.remote_dma(T["rcv%d" % k][:], T["via%d" % k][:], T.sem["arr%d" % k], T.sem.sent, pid, rid, m_out)
-    g.wait_ge(T.sem.sent, nbits(m_out) * len(PIECES))
+    n = 0
+    for k, (w, relay) in enumerate(PIECES):
+        if relay == i:
+            g.wait_ge(T.sem["via_s%d" % k], nbits(m_in))
+            g.remote_dma(T["rcv%d" % k][:], T["via%d" % k][:], T.sem["arr%d" % k], T.sem.sent, pid, rid, m_out)
+            n += nbits(m_out)
+    g.wait_ge(T.sem.sent, n)
 
 
 def rank_program(g, core, T, topo):
     p = plan(T, topo)
     if core in p["relays"]:
-        s, d = p["relays"][core]
-        return run_relay(g, core, T, topo, s, d)
+        s, d, i = p["relays"][core]
+        return run_relay(g, core, T, topo, s, d, i)
     r = T.rank_of(core)
     if r is None:
         return
@@ -84,8 +99,11 @@ def rank_program(g, core, T, topo):
     nb = [cores[(r - 1) % n], cores[(r + 1) % n]]
     far = p["far"][r]
     near = 1 - far
-    hc = LW // 2
     v, S = g.vector, T.sem
+
+    def cols(k, table):
+        half = near if PIECES[k][1] is None else far
+        return table * LW + (half * HALF + START[k]) // LP
 
     g.sync.dma_start(T.li[0:LP, 0:LW], T.snd[:]).then_inc(S.lst, 16)
     g.scalar.dma_start(T.li[0:LP, LW:2 * LW], T.plc[:]).then_inc(S.lst, 16)
@@ -95,6 +113,7 @@ def rank_program(g, core, T, topo):
     g.scalar.dma_start(T.gs[64:128, :], T.gh[64:128, :]).then_inc(S.gld, 16)
 
     g.iota(T.dif[0:LP, :], [[0, 128 // LP], [1, LP]], 0, -1, allow_small_or_imprecise_dtypes=True).then_inc(S.dif_s, 1)
+    v.memset(T.nz[:], -0.0).then_inc(S.nz_s, 1)
     v.wait_ge(S.dif_s, 1)
     v.tensor_scalar(T.rep[0:LP, :], T.dif[0:LP, :], 0.0, None, AluOpType.is_equal).then_inc(S.rep_s, 1)
     v.wait_ge(S.lst, 32)
@@ -107,38 +126,38 @@ def rank_program(g, core, T, topo):
 
     v.wait_ge(S.off_s, 1)
     v.wait_ge(S.xld, 32)
-    o = far * hc
-    for k, w in enumerate(PIECES):
-        v.tensor_copy(T["snd%d" % k][:], T.xs[:, :].indirect(T.offs[:, o:o + w // LP])).then_inc(S["gat%d" % k], 1)
-        o += w // LP
-    v.tensor_copy(T.sdir[:], T.xs[:, :].indirect(T.offs[:, near * hc:(near + 1) * hc])).then_inc(S.gdir, 1)
+    g.scalar.wait_ge(S.nz_s, 1)
+    g.scalar.wait_ge(S.off_s, 1)
+    g.scalar.wait_ge(S.xld, 32)
+    for k, (w, relay) in enumerate(PIECES):
+        o, h = cols(k, 0), w // 2
+        v.tensor_copy(T["snd%d" % k][:, 0:h], T.xs[:, :].indirect(T.offs[:, o:o + h // LP])).then_inc(S["gat%d" % k], 1)
+        g.scalar.activation(T["snd%d" % k][:, h:w], T.xs[:, :].indirect(T.offs[:, o + h // LP:o + w // LP]),
+                            ActivationFunctionType.Identity, bias=T.nz[:, 0:1]).then_inc(S["gat%d" % k], 1)
 
-    via = p["via"][core]
-    rid, pid = topo.addr(via, core)
-    m = topo.mask(core, via)
-    for k in range(len(PIECES)):
-        g.wait_ge(S["gat%d" % k], 1)
-        g.remote_dma(T["via%d" % k][:], T["snd%d" % k][:], S["via_s%d" % k], S.sent, pid, rid, m)
-    rid, pid = topo.addr(nb[near], core)
-    md = topo.mask(core, nb[near])
-    g.wait_ge(S.gdir, 1)
-    g.remote_dma(T.rdir[:], T.sdir[:], S.adir, S.sent, pid, rid, md)
+    sent = 0
+    for k, (w, relay) in enumerate(PIECES):
+        to = nb[near] if relay is None else p["via"][core][relay]
+        land, sem = ("rcv%d", "arr%d") if relay is None else ("via%d", "via_s%d")
+        rid, pid = topo.addr(to, core)
+        m = topo.mask(core, to)
+        g.wait_ge(S["gat%d" % k], 2)
+        g.remote_dma(T[land % k][:], T["snd%d" % k][:], S[sem % k], S.sent, pid, rid, m)
+        sent += nbits(m)
 
     v.wait_ge(S.gld, 32)
-    v.wait_ge(S.adir, nbits(topo.mask(nb[near], core)))
-    v.tensor_copy(T.gs[:, :].indirect(T.offs[:, LW + near * hc:LW + (near + 1) * hc]), T.rdir[:]).then_inc(S.sct, 1)
-    o = LW + far * hc
-    last = p["via"][nb[far]]
-    for k, w in enumerate(PIECES):
+    for j, k in enumerate(SCATTERS):
+        w, relay = PIECES[k]
+        last = nb[near] if relay is None else p["via"][nb[far]][relay]
+        o = cols(k, 1)
         v.wait_ge(S["arr%d" % k], nbits(topo.mask(last, core)))
-        v.wait_ge(S.sct, 1 + k)
+        if j:
+            v.wait_ge(S.sct, j)
         v.tensor_copy(T.gs[:, :].indirect(T.offs[:, o:o + w // LP]), T["rcv%d" % k][:]).then_inc(S.sct, 1)
-        o += w // LP
 
-    done = 1 + len(PIECES)
-    g.sync.wait_ge(S.sct, done)
+    g.sync.wait_ge(S.sct, len(SCATTERS))
     g.sync.dma_start(T.y[0:64, :], T.gs[0:64, :]).then_inc(S.stored, 16)
-    g.scalar.wait_ge(S.sct, done)
+    g.scalar.wait_ge(S.sct, len(SCATTERS))
     g.scalar.dma_start(T.y[64:128, :], T.gs[64:128, :]).then_inc(S.stored, 16)
-    g.wait_ge(S.sent, nbits(m) * len(PIECES) + nbits(md))
+    g.wait_ge(S.sent, sent)
     g.wait_ge(S.stored, 32)

@@ -1,41 +1,53 @@
 import numpy as np
+from concourse.bass import DstId, RemoteDMATransfer
 from concourse.mybir import dt, AluOpType, ActivationFunctionType
 
-PIECES = [(128, 0), (192, 1), (320, None), (192, 0), (192, None)]
-SCATTERS = [2, 4, 0, 1, 3]
+PIECES = [(128, 0), (128, 1), (320, None), (128, 0), (128, 1), (192, None)]
+WRITES = [[0], [1], [2], [3, 4], [5]]
+SCATTERS = [[2], [5], [0, 1], [3, 4]]
 XC, HALF, LP, LW = 4096, 512, 16, 64
 ALL_CORES = 512
-RELAYS = 2
 
 SCRATCH = {
     "xs": ("sbuf", [128, XC], "bfloat16"),
     "gs": ("sbuf", [128, XC], "bfloat16"),
-    "li": ("sbuf", [128, 2 * LW], "int32"),
-    "lf": ("sbuf", [128, 2 * LW], "float32"),
-    "offs": ("sbuf", [128, 2 * LW], "uint16"),
+    "snd_far": ("sbuf", [128, HALF], "bfloat16"),
+    "snd_near": ("sbuf", [128, HALF], "bfloat16"),
+    "via": ("sbuf", [128, HALF], "bfloat16"),
+    "rcv_far": ("sbuf", [128, HALF], "bfloat16"),
+    "rcv_near": ("sbuf", [128, HALF], "bfloat16"),
+    "nz": ("sbuf", [128, 1], "float32"),
     "dif": ("sbuf", [128, 128], "float32"),
     "rep": ("sbuf", [128, 128], "float32"),
-    "nz": ("sbuf", [128, 1], "float32"),
-    "pl": ("psum", [128, 512], "float32"),
 }
-SEMAPHORES = ["lst", "xld", "gld", "dif_s", "rep_s", "lf_s", "pl_s", "off_s", "nz_s", "sct", "sent", "stored"]
+SEMAPHORES = ["xld", "gld", "dif_s", "rep_s", "nz_s", "sct", "sent", "stored"]
+for _t in ("a", "b"):
+    SCRATCH["li_" + _t] = ("sbuf", [128, LW], "int32")
+    SCRATCH["lf_" + _t] = ("sbuf", [128, LW], "float32")
+    SCRATCH["off_" + _t] = ("sbuf", [128, LW], "uint16")
+    SCRATCH["ps_" + _t] = ("psum", [128, 512], "float32")
+    SEMAPHORES += ["ld_" + _t, "cv_" + _t, "mm_" + _t, "ok_" + _t]
+SEMAPHORES += ["gat%d" % _i for _i in range(len(WRITES))]
 START = []
 _at = {True: 0, False: 0}
 for _k, (_w, _r) in enumerate(PIECES):
     START.append(_at[_r is None])
     _at[_r is None] += _w
-    SCRATCH["snd%d" % _k] = ("sbuf", [128, _w], "bfloat16")
-    SCRATCH["rcv%d" % _k] = ("sbuf", [128, _w], "bfloat16")
-    SEMAPHORES += ["gat%d" % _k, "arr%d" % _k]
-    if _r is not None:
-        SCRATCH["via%d" % _k] = ("sbuf", [128, _w], "bfloat16")
-        SEMAPHORES.append("via_s%d" % _k)
+    SEMAPHORES += ["via_s%d" % _k, "arr%d" % _k]
 
 _PLAN = {}
 
 
 def nbits(m):
     return bin(m).count("1")
+
+
+def engines(m, k):
+    for call in WRITES:
+        if k in call:
+            bits = [b for b in range(m.bit_length()) if (m >> b) & 1]
+            each, i = len(bits) // len(call), call.index(k)
+            return sum(1 << b for b in bits[i * each:(i + 1) * each])
 
 
 def relays_for(s, d, T, topo):
@@ -80,8 +92,9 @@ def run_relay(g, core, T, topo, s, d, i):
     n = 0
     for k, (w, relay) in enumerate(PIECES):
         if relay == i:
-            g.wait_ge(T.sem["via_s%d" % k], nbits(m_in))
-            g.remote_dma(T["rcv%d" % k][:], T["via%d" % k][:], T.sem["arr%d" % k], T.sem.sent, pid, rid, m_out)
+            a, b = START[k], START[k] + w
+            g.wait_ge(T.sem["via_s%d" % k], nbits(engines(m_in, k)))
+            g.remote_dma(T.rcv_far[:, a:b], T.via[:, a:b], T.sem["arr%d" % k], T.sem.sent, pid, rid, m_out)
             n += nbits(m_out)
     g.wait_ge(T.sem.sent, n)
 
@@ -101,59 +114,83 @@ def rank_program(g, core, T, topo):
     near = 1 - far
     v, S = g.vector, T.sem
 
-    def cols(k, table):
-        half = near if PIECES[k][1] is None else far
-        return table * LW + (half * HALF + START[k]) // LP
+    def span(ks):
+        a, w = START[ks[0]], sum(PIECES[k][0] for k in ks)
+        return a, w, ((near if PIECES[ks[0]][1] is None else far) * HALF + a) // LP
 
-    g.sync.dma_start(T.li[0:LP, 0:LW], T.snd[:]).then_inc(S.lst, 16)
-    g.scalar.dma_start(T.li[0:LP, LW:2 * LW], T.plc[:]).then_inc(S.lst, 16)
     g.sync.dma_start(T.xs[0:64, :], T.x[0:64, :]).then_inc(S.xld, 16)
+    g.scalar.dma_start(T.li_a[0:LP, :], T.snd[:]).then_inc(S.ld_a, 16)
     g.scalar.dma_start(T.xs[64:128, :], T.x[64:128, :]).then_inc(S.xld, 16)
-    g.sync.dma_start(T.gs[0:64, :], T.gh[0:64, :]).then_inc(S.gld, 16)
+    g.sync.dma_start(T.li_b[0:LP, :], T.plc[:]).then_inc(S.ld_b, 16)
     g.scalar.dma_start(T.gs[64:128, :], T.gh[64:128, :]).then_inc(S.gld, 16)
+    g.sync.dma_start(T.gs[0:64, :], T.gh[0:64, :]).then_inc(S.gld, 16)
 
     g.iota(T.dif[0:LP, :], [[0, 128 // LP], [1, LP]], 0, -1, allow_small_or_imprecise_dtypes=True).then_inc(S.dif_s, 1)
     v.memset(T.nz[:], -0.0).then_inc(S.nz_s, 1)
     v.wait_ge(S.dif_s, 1)
     v.tensor_scalar(T.rep[0:LP, :], T.dif[0:LP, :], 0.0, None, AluOpType.is_equal).then_inc(S.rep_s, 1)
-    v.wait_ge(S.lst, 32)
-    v.tensor_copy(T.lf[0:LP, :], T.li[0:LP, :]).then_inc(S.lf_s, 1)
     g.tensor.wait_ge(S.rep_s, 1)
-    g.tensor.wait_ge(S.lf_s, 1)
-    g.tensor.matmul(T.pl[:, 0:2 * LW], T.rep[0:LP, :], T.lf[0:LP, :], True, True).then_inc(S.pl_s, 1)
-    v.wait_ge(S.pl_s, 1)
-    v.tensor_copy(T.offs[:], T.pl[:, 0:2 * LW]).then_inc(S.off_s, 1)
 
-    v.wait_ge(S.off_s, 1)
+    def offsets(t):
+        v.wait_ge(S["ld_" + t], 16)
+        v.tensor_copy(T["lf_" + t][0:LP, :], T["li_" + t][0:LP, :]).then_inc(S["cv_" + t], 1)
+        g.tensor.wait_ge(S["cv_" + t], 1)
+        g.tensor.matmul(T["ps_" + t][:, 0:LW], T.rep[0:LP, :], T["lf_" + t][0:LP, :], True, True).then_inc(S["mm_" + t], 1)
+        v.wait_ge(S["mm_" + t], 1)
+        v.tensor_copy(T["off_" + t][:], T["ps_" + t][:, 0:LW]).then_inc(S["ok_" + t], 1)
+        v.wait_ge(S["ok_" + t], 1)
+
+    offsets("a")
     v.wait_ge(S.xld, 32)
     g.scalar.wait_ge(S.nz_s, 1)
-    g.scalar.wait_ge(S.off_s, 1)
+    g.scalar.wait_ge(S.ok_a, 1)
     g.scalar.wait_ge(S.xld, 32)
-    for k, (w, relay) in enumerate(PIECES):
-        o, h = cols(k, 0), w // 2
-        v.tensor_copy(T["snd%d" % k][:, 0:h], T.xs[:, :].indirect(T.offs[:, o:o + h // LP])).then_inc(S["gat%d" % k], 1)
-        g.scalar.activation(T["snd%d" % k][:, h:w], T.xs[:, :].indirect(T.offs[:, o + h // LP:o + w // LP]),
-                            ActivationFunctionType.Identity, bias=T.nz[:, 0:1]).then_inc(S["gat%d" % k], 1)
+    for i, ks in enumerate(WRITES):
+        a, w, o = span(ks)
+        h = w // 2
+        buf = T.snd_near if PIECES[ks[0]][1] is None else T.snd_far
+        v.tensor_copy(buf[:, a:a + h], T.xs[:, :].indirect(T.off_a[:, o:o + h // LP])).then_inc(S["gat%d" % i], 1)
+        g.scalar.activation(buf[:, a + h:a + w], T.xs[:, :].indirect(T.off_a[:, o + h // LP:o + w // LP]),
+                            ActivationFunctionType.Identity, bias=T.nz[:, 0:1]).then_inc(S["gat%d" % i], 1)
 
     sent = 0
-    for k, (w, relay) in enumerate(PIECES):
-        to = nb[near] if relay is None else p["via"][core][relay]
-        land, sem = ("rcv%d", "arr%d") if relay is None else ("via%d", "via_s%d")
-        rid, pid = topo.addr(to, core)
-        m = topo.mask(core, to)
-        g.wait_ge(S["gat%d" % k], 2)
-        g.remote_dma(T[land % k][:], T["snd%d" % k][:], S[sem % k], S.sent, pid, rid, m)
-        sent += nbits(m)
+    for i, ks in enumerate(WRITES):
+        g.wait_ge(S["gat%d" % i], 2)
+        calls = []
+        for k in ks:
+            w, relay = PIECES[k]
+            a, b = START[k], START[k] + w
+            if relay is None:
+                to, src, dst, sem = nb[near], T.snd_near, T.rcv_near, S["arr%d" % k]
+            else:
+                to, src, dst, sem = p["via"][core][relay], T.snd_far, T.via, S["via_s%d" % k]
+            rid, pid = topo.addr(to, core)
+            m = engines(topo.mask(core, to), k)
+            sent += nbits(m)
+            calls.append((dst[:, a:b], src[:, a:b], sem, pid, rid, m))
+        if len(calls) == 1:
+            dst, src, sem, pid, rid, m = calls[0]
+            g.remote_dma(dst, src, sem, S.sent, pid, rid, m)
+        else:
+            g.remote_dma_fused([RemoteDMATransfer(dst_ids=[DstId(rid=rid, pnc=pid)], dma_engine_mask=m, remote_sem=sem,
+                                                  src=src, dst=dst) for dst, src, sem, pid, rid, m in calls],
+                               local_sem=S.sent)
 
+    offsets("b")
     v.wait_ge(S.gld, 32)
-    for j, k in enumerate(SCATTERS):
-        w, relay = PIECES[k]
-        last = nb[near] if relay is None else p["via"][nb[far]][relay]
-        o = cols(k, 1)
-        v.wait_ge(S["arr%d" % k], nbits(topo.mask(last, core)))
+    for j, ks in enumerate(SCATTERS):
+        a, w, o = span(ks)
+        for k in ks:
+            relay = PIECES[k][1]
+            if relay is None:
+                count = nbits(engines(topo.mask(nb[near], core), k))
+            else:
+                count = nbits(topo.mask(p["via"][nb[far]][relay], core))
+            v.wait_ge(S["arr%d" % k], count)
         if j:
             v.wait_ge(S.sct, j)
-        v.tensor_copy(T.gs[:, :].indirect(T.offs[:, o:o + w // LP]), T["rcv%d" % k][:]).then_inc(S.sct, 1)
+        buf = T.rcv_near if PIECES[ks[0]][1] is None else T.rcv_far
+        v.tensor_copy(T.gs[:, :].indirect(T.off_b[:, o:o + w // LP]), buf[:, a:a + w]).then_inc(S.sct, 1)
 
     g.sync.wait_ge(S.sct, len(SCATTERS))
     g.sync.dma_start(T.y[0:64, :], T.gs[0:64, :]).then_inc(S.stored, 16)

import numpy as np
from concourse.bass import DstId, RemoteDMATransfer
from concourse.mybir import dt, AluOpType, ActivationFunctionType

PIECES = [(128, 0), (128, 1), (320, None), (128, 0), (128, 1), (192, None)]
WRITES = [[0], [1], [2], [3, 4], [5]]
SCATTERS = [[2], [5], [0, 1], [3, 4]]
XC, HALF, LP, LW = 4096, 512, 16, 64
ALL_CORES = 512

SCRATCH = {
    "xs": ("sbuf", [128, XC], "bfloat16"),
    "gs": ("sbuf", [128, XC], "bfloat16"),
    "snd_far": ("sbuf", [128, HALF], "bfloat16"),
    "snd_near": ("sbuf", [128, HALF], "bfloat16"),
    "via": ("sbuf", [128, HALF], "bfloat16"),
    "rcv_far": ("sbuf", [128, HALF], "bfloat16"),
    "rcv_near": ("sbuf", [128, HALF], "bfloat16"),
    "nz": ("sbuf", [128, 1], "float32"),
    "dif": ("sbuf", [128, 128], "float32"),
    "rep": ("sbuf", [128, 128], "float32"),
}
SEMAPHORES = ["xld", "gld", "dif_s", "rep_s", "nz_s", "sct", "sent", "stored"]
for _t in ("a", "b"):
    SCRATCH["li_" + _t] = ("sbuf", [128, LW], "int32")
    SCRATCH["lf_" + _t] = ("sbuf", [128, LW], "float32")
    SCRATCH["off_" + _t] = ("sbuf", [128, LW], "uint16")
    SCRATCH["ps_" + _t] = ("psum", [128, 512], "float32")
    SEMAPHORES += ["ld_" + _t, "cv_" + _t, "mm_" + _t, "ok_" + _t]
SEMAPHORES += ["gat%d" % _i for _i in range(len(WRITES))]
START = []
_at = {True: 0, False: 0}
for _k, (_w, _r) in enumerate(PIECES):
    START.append(_at[_r is None])
    _at[_r is None] += _w
    SEMAPHORES += ["via_s%d" % _k, "arr%d" % _k]

_PLAN = {}


def nbits(m):
    return bin(m).count("1")


def engines(m, k):
    for call in WRITES:
        if k in call:
            bits = [b for b in range(m.bit_length()) if (m >> b) & 1]
            each, i = len(bits) // len(call), call.index(k)
            return sum(1 << b for b in bits[i * each:(i + 1) * each])


def relays_for(s, d, T, topo):
    found = [None, None]
    for c in range(ALL_CORES):
        if topo.host(c) == topo.host(s) or topo.rack(topo.host(c)) != topo.rack(topo.host(s)):
            continue
        if T.rank_of(c) is not None or topo.chip(c) != topo.chip(d):
            continue
        if not (topo.may_write(s, c) and topo.may_write(c, d)):
            continue
        if any(topo.mates(c, q) and topo.may_write(c, q) for q in range(ALL_CORES)):
            continue
        i = 0 if topo.die(c) == topo.die(s) else 1
        if found[i] is None:
            found[i] = c
    assert found[0] is not None and found[1] is not None
    return found


def plan(T, topo):
    if not _PLAN:
        cores = list(T.cores)
        n = len(cores)
        _PLAN["relays"], _PLAN["via"], _PLAN["far"] = {}, {}, {}
        for r, s in enumerate(cores):
            nb = [cores[(r - 1) % n], cores[(r + 1) % n]]
            far = [k for k in (0, 1) if not topo.may_write(s, nb[k])]
            assert len(far) == 1
            via = relays_for(s, nb[far[0]], T, topo)
            _PLAN["far"][r] = far[0]
            _PLAN["via"][s] = via
            for i, c in enumerate(via):
                assert c not in _PLAN["relays"]
                _PLAN["relays"][c] = (s, nb[far[0]], i)
    return _PLAN


def run_relay(g, core, T, topo, s, d, i):
    rid, pid = topo.addr(d, core)
    m_in, m_out = topo.mask(s, core), topo.mask(core, d)
    n = 0
    for k, (w, relay) in enumerate(PIECES):
        if relay == i:
            a, b = START[k], START[k] + w
            g.wait_ge(T.sem["via_s%d" % k], nbits(engines(m_in, k)))
            g.remote_dma(T.rcv_far[:, a:b], T.via[:, a:b], T.sem["arr%d" % k], T.sem.sent, pid, rid, m_out)
            n += nbits(m_out)
    g.wait_ge(T.sem.sent, n)


def rank_program(g, core, T, topo):
    p = plan(T, topo)
    if core in p["relays"]:
        s, d, i = p["relays"][core]
        return run_relay(g, core, T, topo, s, d, i)
    r = T.rank_of(core)
    if r is None:
        return
    cores = list(T.cores)
    n = len(cores)
    nb = [cores[(r - 1) % n], cores[(r + 1) % n]]
    far = p["far"][r]
    near = 1 - far
    v, S = g.vector, T.sem

    def span(ks):
        a, w = START[ks[0]], sum(PIECES[k][0] for k in ks)
        return a, w, ((near if PIECES[ks[0]][1] is None else far) * HALF + a) // LP

    g.sync.dma_start(T.xs[0:64, :], T.x[0:64, :]).then_inc(S.xld, 16)
    g.scalar.dma_start(T.li_a[0:LP, :], T.snd[:]).then_inc(S.ld_a, 16)
    g.scalar.dma_start(T.xs[64:128, :], T.x[64:128, :]).then_inc(S.xld, 16)
    g.sync.dma_start(T.li_b[0:LP, :], T.plc[:]).then_inc(S.ld_b, 16)
    g.scalar.dma_start(T.gs[64:128, :], T.gh[64:128, :]).then_inc(S.gld, 16)
    g.sync.dma_start(T.gs[0:64, :], T.gh[0:64, :]).then_inc(S.gld, 16)

    g.iota(T.dif[0:LP, :], [[0, 128 // LP], [1, LP]], 0, -1, allow_small_or_imprecise_dtypes=True).then_inc(S.dif_s, 1)
    v.memset(T.nz[:], -0.0).then_inc(S.nz_s, 1)
    v.wait_ge(S.dif_s, 1)
    v.tensor_scalar(T.rep[0:LP, :], T.dif[0:LP, :], 0.0, None, AluOpType.is_equal).then_inc(S.rep_s, 1)
    g.tensor.wait_ge(S.rep_s, 1)

    def offsets(t):
        v.wait_ge(S["ld_" + t], 16)
        v.tensor_copy(T["lf_" + t][0:LP, :], T["li_" + t][0:LP, :]).then_inc(S["cv_" + t], 1)
        g.tensor.wait_ge(S["cv_" + t], 1)
        g.tensor.matmul(T["ps_" + t][:, 0:LW], T.rep[0:LP, :], T["lf_" + t][0:LP, :], True, True).then_inc(S["mm_" + t], 1)
        v.wait_ge(S["mm_" + t], 1)
        v.tensor_copy(T["off_" + t][:], T["ps_" + t][:, 0:LW]).then_inc(S["ok_" + t], 1)
        v.wait_ge(S["ok_" + t], 1)

    offsets("a")
    v.wait_ge(S.xld, 32)
    g.scalar.wait_ge(S.nz_s, 1)
    g.scalar.wait_ge(S.ok_a, 1)
    g.scalar.wait_ge(S.xld, 32)
    for i, ks in enumerate(WRITES):
        a, w, o = span(ks)
        h = w // 2
        buf = T.snd_near if PIECES[ks[0]][1] is None else T.snd_far
        v.tensor_copy(buf[:, a:a + h], T.xs[:, :].indirect(T.off_a[:, o:o + h // LP])).then_inc(S["gat%d" % i], 1)
        g.scalar.activation(buf[:, a + h:a + w], T.xs[:, :].indirect(T.off_a[:, o + h // LP:o + w // LP]),
                            ActivationFunctionType.Identity, bias=T.nz[:, 0:1]).then_inc(S["gat%d" % i], 1)

    sent = 0
    for i, ks in enumerate(WRITES):
        g.wait_ge(S["gat%d" % i], 2)
        calls = []
        for k in ks:
            w, relay = PIECES[k]
            a, b = START[k], START[k] + w
            if relay is None:
                to, src, dst, sem = nb[near], T.snd_near, T.rcv_near, S["arr%d" % k]
            else:
                to, src, dst, sem = p["via"][core][relay], T.snd_far, T.via, S["via_s%d" % k]
            rid, pid = topo.addr(to, core)
            m = engines(topo.mask(core, to), k)
            sent += nbits(m)
            calls.append((dst[:, a:b], src[:, a:b], sem, pid, rid, m))
        if len(calls) == 1:
            dst, src, sem, pid, rid, m = calls[0]
            g.remote_dma(dst, src, sem, S.sent, pid, rid, m)
        else:
            g.remote_dma_fused([RemoteDMATransfer(dst_ids=[DstId(rid=rid, pnc=pid)], dma_engine_mask=m, remote_sem=sem,
                                                  src=src, dst=dst) for dst, src, sem, pid, rid, m in calls],
                               local_sem=S.sent)

    offsets("b")
    v.wait_ge(S.gld, 32)
    for j, ks in enumerate(SCATTERS):
        a, w, o = span(ks)
        for k in ks:
            relay = PIECES[k][1]
            if relay is None:
                count = nbits(engines(topo.mask(nb[near], core), k))
            else:
                count = nbits(topo.mask(p["via"][nb[far]][relay], core))
            v.wait_ge(S["arr%d" % k], count)
        if j:
            v.wait_ge(S.sct, j)
        buf = T.rcv_near if PIECES[ks[0]][1] is None else T.rcv_far
        v.tensor_copy(T.gs[:, :].indirect(T.off_b[:, o:o + w // LP]), buf[:, a:a + w]).then_inc(S.sct, 1)

    g.sync.wait_ge(S.sct, len(SCATTERS))
    g.sync.dma_start(T.y[0:64, :], T.gs[0:64, :]).then_inc(S.stored, 16)
    g.scalar.wait_ge(S.sct, len(SCATTERS))
    g.scalar.dma_start(T.y[64:128, :], T.gs[64:128, :]).then_inc(S.stored, 16)
    g.wait_ge(S.sent, sent)
    g.wait_ge(S.stored, 32)
